import numpy as np
import ml_dtypes


def mxq(x, axis, fmt="e4m3"):
    dtype, down = {"e4m3": (ml_dtypes.float8_e4m3fn, 7), "e5m2": (ml_dtypes.float8_e5m2, 14)}[fmt]
    v = np.moveaxis(np.asarray(x, np.float32).astype(ml_dtypes.bfloat16).astype(np.float64), axis, -1)
    blocks = v.reshape(v.shape[:-1] + (-1, 32))
    amax = np.abs(blocks).max(-1, keepdims=True)
    byte = np.maximum(np.where(amax > 0, np.frexp(amax)[1] - 1 + 127, 0) - down, 1)
    scale = np.exp2(byte - 127.0)
    codes = (blocks / scale).astype(np.float32).astype(dtype).astype(np.float64)
    return np.moveaxis((codes * scale).reshape(v.shape), -1, axis)


WIDE = False


def mx_kscale(k):
    if not WIDE:
        return np.ones(k)
    levels = np.array([30, -30])
    if k % 512:
        return np.exp2(np.random.permutation(np.resize(levels, k // 32))).repeat(32)
    a = np.empty((k // 512, 16))
    for p in range(k // 512):
        a[p, :8] = np.random.permutation(np.resize(levels, 8))
        for g in range(8):
            far = levels[np.abs(levels - a[p, g]) >= 10]
            a[p, g + 8] = far[np.random.randint(len(far))]
    return np.exp2(a.ravel()).repeat(32)


def f64(x):
    return np.asarray(x).astype(np.float64)


def striped(idx):
    return np.tile(np.asarray(idx).reshape(-1, 16).T, (8, 1)).astype(np.uint16)


def unstriped(offs):
    return offs[:16].T.reshape(-1).astype(np.int64)


E2M1 = np.array([0.0, 0.5, 1.0, 1.5, 2.0, 3.0, 4.0, 6.0, -0.0, -0.5, -1.0, -1.5, -2.0, -3.0, -4.0, -6.0])


def pack_weight(w, fmt):
    k, n = w.shape
    w = f64(np.asarray(w, np.float32).astype(ml_dtypes.bfloat16)).reshape(k // 32, 32, n)
    amax = np.abs(w).max(1)
    if fmt in ("e4m3", "e5m2"):
        byte = np.frexp(amax)[1] - 1 + 127 - (7 if fmt == "e4m3" else 14)
    else:
        mant, ex = np.frexp(amax / 6.0)
        byte = np.where(mant > 0.5, ex, ex - 1) + 127
    byte = np.clip(np.where(amax > 0, byte, 1), 1, 254)
    scaled = (w * np.exp2(127.0 - byte)[:, None, :]).reshape(k, n).astype(np.float32)
    by_word = np.ascontiguousarray(scaled.reshape(k // 512, 128, 4, n).transpose(0, 1, 3, 2))
    if fmt in ("e4m3", "e5m2"):
        words = by_word.astype(ml_dtypes.float8_e4m3fn if fmt == "e4m3" else ml_dtypes.float8_e5m2).view(np.uint8)
    else:
        c = by_word.astype(ml_dtypes.float4_e2m1fn).view(np.uint8) & 0xF
        words = (c[..., 0::2] | (c[..., 1::2] << 4)).reshape(k // 512, 128, 2 * n)
    return np.ascontiguousarray(words), np.ascontiguousarray(byte.astype(np.uint8).reshape(k // 512, 16, n))


def unpack_weight(words, scales, fmt):
    g, _, n = scales.shape
    words = np.ascontiguousarray(words).reshape(g, 128, n, -1)
    if fmt in ("e4m3", "e5m2"):
        vals = words.view(ml_dtypes.float8_e4m3fn if fmt == "e4m3" else ml_dtypes.float8_e5m2).astype(np.float64)
    else:
        nib = np.empty((g, 128, n, 4), np.uint8)
        nib[..., 0::2] = words & 0xF
        nib[..., 1::2] = words >> 4
        vals = E2M1[nib]
    vals = vals * np.repeat(np.exp2(scales.astype(np.float64) - 127.0), 8, axis=1)[..., None]
    return vals.transpose(0, 1, 3, 2).reshape(g * 512, n)


def bf(x):
    return np.asarray(x, np.float32).astype(ml_dtypes.bfloat16)


def planes(Y):
    r, m = Y.shape
    b = f64(bf(Y)).reshape(r // 32, 32, m)
    amax = np.abs(b).max(1)
    byte = np.clip(np.where(amax > 0, np.frexp(amax)[1] - 1 + 127 - 7, 1), 1, 254)
    codes = (b * np.exp2(127.0 - byte)[:, None, :]).reshape(r, m).astype(np.float32).astype(ml_dtypes.float8_e4m3fn).view(np.uint8)
    words = codes.reshape(r // 512, 128, 4, m).transpose(0, 1, 3, 2)
    return np.ascontiguousarray(words), np.ascontiguousarray(byte.astype(np.uint8).reshape(r // 512, 16, m))


K, T, J, S, R, O, N = 512, 512, 256, 512, 512, 128, 512


def setup_inputs():
    n = np.random.standard_normal
    idx = np.random.permutation(T)[:J]
    idx2 = np.random.permutation(S)[:J]
    idx3 = np.random.permutation(J)[:O]
    idx4 = np.random.permutation(J)[:O]
    fk = mx_kscale(K)
    fr = mx_kscale(R)
    wp = pack_weight(n((K, R)) * 1 / np.sqrt(K) * fk[:, None] * fr, "e5m2")
    wbp = pack_weight(n((R, N)) * 1 / np.sqrt(R) / fr[:, None], "e4m3")
    return {
        "xa": (n((K, T))).astype(np.float32),
        "xb": (n((K, S))).astype(np.float32),
        "hb": (np.random.uniform(0.2, 0.9, (K, 1))).astype(np.float32),
        "fk": (np.random.uniform(0.5, 2.0, (K, 1)) / fk[:, None]).astype(np.float32),
        "w_words": wp[0],
        "w_scales": wp[1],
        "wb_words": wbp[0],
        "wb_scales": wbp[1],
        "rs": (n((N, O))).astype(np.float32),
        "gm": (np.random.uniform(0.5, 2.0, (N, 1))).astype(np.float32),
        "offs": striped(idx),
        "offs2": striped(idx2),
        "offs3": striped(idx3),
        "offs4": striped(idx4),
    }


def reference(xa, xb, hb, fk, w_words, w_scales, wb_words, wb_scales, rs, gm, offs, offs2, offs3, offs4):
    idx = unstriped(offs)
    idx2 = unstriped(offs2)
    idx3 = unstriped(offs3)
    idx4 = unstriped(offs4)
    wu = unpack_weight(w_words, w_scales, "e5m2")
    wbu = unpack_weight(wb_words, wb_scales, "e4m3")
    u = (f64(xa)[:, idx] - np.minimum(f64(xb)[:, idx2], f64(hb))) * f64(fk)
    uq = mxq(u, 0, "e5m2")
    a = wu.T @ uq
    ha = np.maximum(a, 0.0)
    hid = ha[:, idx3] - ha[:, idx4]
    hidq = mxq(hid, 0, "e5m2")
    p = wbu.T @ hidq
    y = f64(gm) * p + f64(rs)
    words, scales = planes(y)
    return y, words, scales

@@ -1,0 +1,172 @@
+from contextlib import ExitStack
+
+import concourse.mybir as mybir
+
+K, T, J, S, R, O, N = 512, 512, 256, 512, 512, 128, 512
+FLOPS = 2 * K * R * J + 2 * R * N * O
+
+F32 = mybir.dt.float32
+BF16 = mybir.dt.bfloat16
+I32 = mybir.dt.int32
+U32 = mybir.dt.uint32
+U16 = mybir.dt.uint16
+U8 = mybir.dt.uint8
+E4M3 = mybir.dt.float8_e4m3fn_x4
+E5M2 = mybir.dt.float8_e5m2_x4
+ALU = mybir.AluOpType
+ACT = mybir.ActivationFunctionType
+
+P = 128
+PACK = 4
+QUADS = 4
+HALF = J // 2
+COLS = HALF // 16
+
+
+def tile_list_looks_boundedgaps_gap_residual_pl_kernel(
+    tc, xa, xb, hb, fk, w_words, w_scales, wb_words, wb_scales, rs, gm, offs, offs2, offs3, offs4, out_0, out_1, out_2
+):
+    nc = tc.nc
+    with ExitStack() as ctx:
+        sb = ctx.enter_context(tc.tile_pool(name="sb", bufs=1))
+        ps = ctx.enter_context(tc.psum_pool(name="ps", bufs=1))
+
+        def tile(shape, dtype, name):
+            return sb.tile(shape, dtype, name=name, align_bytes=64)
+
+        def dealt(ap):
+            return ap.rearrange("(p t) c -> p t c", t=PACK)
+
+        def load_scales(queue, dst, src):
+            for q in range(QUADS):
+                queue.dma_start(out=dst[32 * q : 32 * q + 4, :].bitcast(I32), in_=src[0, 4 * q : 4 * q + 4, :].bitcast(I32))
+
+        def load_words(dst, src):
+            nc.sync.dma_start(out=dst[:].bitcast(I32), in_=src[0].rearrange("p c t -> p (c t)").bitcast(I32))
+
+        def deal_words(dst, src):
+            nc.scalar.copy(out=dst[:].rearrange("p (t m) -> p m t", t=PACK), in_=src[:].rearrange("p (m t) -> p m t", t=PACK))
+
+        def deal_scales(dst, src):
+            nc.vector.tensor_copy(out=dst[:].rearrange("p (t m) -> p t m", t=PACK), in_=src[:].rearrange("p (m t) -> p t m", t=PACK))
+
+        la = tile([P, J // 16], U16, "la")
+        lb = tile([P, J // 16], U16, "lb")
+        l3 = tile([P, O // 16], U16, "l3")
+        l4 = tile([P, O // 16], U16, "l4")
+        xa_sb = [tile([P, T], F32, "xa%d" % t) for t in range(PACK)]
+        xb_sb = [tile([P, S], F32, "xb%d" % t) for t in range(PACK)]
+        hb_sb = tile([P, PACK], F32, "hb_sb")
+        fk_sb = tile([P, PACK], F32, "fk_sb")
+        gm_sb = tile([P, PACK], F32, "gm_sb")
+        rs_sb = tile([P, PACK, O], F32, "rs_sb")
+        w_raw = tile([P, R], U32, "w_raw")
+        wb_raw = tile([P, N], U32, "wb_raw")
+        ws_raw = tile([P, R], U8, "ws_raw")
+        wbs_raw = tile([P, N], U8, "wbs_raw")
+        w_c = tile([P, R], U32, "w_c")
+        wb_c = tile([P, N], U32, "wb_c")
+        w_s = tile([P, R], U8, "w_s")
+        wb_s = tile([P, N], U8, "wb_s")
+
+        nc.vector.memset(ws_raw[:].bitcast(I32), 0)
+        nc.vector.memset(wbs_raw[:].bitcast(I32), 0)
+
+        def load_vec(queue, dst, src):
+            queue.dma_start(out=dst[:], in_=src.rearrange("(p t) c -> p (t c)", t=PACK))
+
+        load_vec(nc.gpsimd, gm_sb, gm)
+        for t in range(PACK):
+            if t == PACK - 1:
+                load_scales(nc.sync, ws_raw, w_scales)
+            nc.sync.dma_start(out=xb_sb[t][:], in_=dealt(xb)[:, t, :])
+            if t == 0:
+                nc.sync.dma_start(lb[:], offs2)
+            nc.sync.dma_start(out=xa_sb[t][:], in_=dealt(xa)[:, t, :])
+            if t == 0:
+                nc.sync.dma_start(la[:], offs)
+                load_vec(nc.sync, hb_sb, hb)
+                load_vec(nc.sync, fk_sb, fk)
+        load_words(w_raw, w_words)
+        nc.sync.dma_start(l3[:], offs3)
+        nc.sync.dma_start(l4[:], offs4)
+        load_scales(nc.sync, wbs_raw, wb_scales)
+        load_words(wb_raw, wb_words)
+        nc.sync.dma_start(out=rs_sb[:], in_=dealt(rs))
+
+        u_bf = [tile([P, HALF, PACK], BF16, "u_bf%d" % h) for h in range(2)]
+        for t in range(PACK):
+            gb = tile([P, J], F32, "gb%d" % t)
+            nc.scalar.activation(gb[:], xb_sb[t][:].indirect(lb[:]), ACT.Copy)
+            ga = [tile([P, HALF], F32, "ga%d_%d" % (t, h)) for h in range(2)]
+            nc.scalar.activation(ga[0][:], xa_sb[t][:].indirect(la[:, 0:COLS]), ACT.Copy)
+            if t % 2 == 1:
+                nc.vector.tensor_copy(ga[1][:], xa_sb[t][:].indirect(la[:, COLS : 2 * COLS]))
+            else:
+                nc.scalar.activation(ga[1][:], xa_sb[t][:].indirect(la[:, COLS : 2 * COLS]), ACT.Copy)
+            neg = [tile([P, HALF], F32, "neg%d_%d" % (t, h)) for h in range(2)]
+            for h in range(2):
+                nc.vector.scalar_tensor_tensor(
+                    neg[h][:], gb[:, h * HALF : (h + 1) * HALF], hb_sb[:, t : t + 1], ga[h][:], ALU.min, ALU.subtract
+                )
+            for h in range(2):
+                nc.vector.tensor_scalar(u_bf[h][:, :, t], neg[h][:], fk_sb[:, t : t + 1], -1.0, ALU.mult, ALU.mult)
+            if t == PACK - 2:
+                deal_scales(w_s, ws_raw)
+        deal_words(w_c, w_raw)
+        u_c = [tile([P, HALF], U32, "u_c%d" % h) for h in range(2)]
+        u_s = [tile([P, HALF], U8, "u_s%d" % h) for h in range(2)]
+        for h in range(2):
+            nc.vector.quantize_mx(out=u_c[h][:].bitcast(E5M2), scales=u_s[h][:], in_=u_bf[h][:].rearrange("p j t -> p (j t)"))
+        deal_scales(wb_s, wbs_raw)
+        deal_words(wb_c, wb_raw)
+
+        g3 = tile([P, PACK, O], F32, "g3")
+        g4 = tile([P, PACK, O], F32, "g4")
+        for t in range(PACK):
+            cols = slice(t * P, (t + 1) * P)
+            ha = tile([P, J], F32, "ha%d" % t)
+            for h in range(2):
+                acc = ps.tile([P, HALF], F32, name="acc%d_%d" % (t, h), tag="bank%d" % (2 * t + h))
+                nc.tensor.matmul_mx(
+                    out=acc[:], lhsT=w_c[:, cols].bitcast(E5M2), lhsT_scale=w_s[:, cols],
+                    rhs=u_c[h][:].bitcast(E5M2), rhs_scale=u_s[h][:], start=True, stop=True,
+                )
+                if h == 0:
+                    nc.vector.tensor_scalar_max(ha[:, 0:HALF], acc[:], 0.0)
+                else:
+                    nc.scalar.activation(ha[:, HALF:J], acc[:], ACT.Relu)
+            nc.vector.tensor_copy(g3[:, t, :], ha[:].indirect(l3[:]))
+            nc.scalar.activation(g4[:, t, :], ha[:].indirect(l4[:]), ACT.Copy)
+        h_bf = tile([P, O, PACK], BF16, "h_bf")
+        nc.vector.tensor_tensor(
+            h_bf[:].rearrange("p (c i) t -> p c t i", i=4),
+            g3[:].rearrange("p t (c i) -> p c t i", i=4),
+            g4[:].rearrange("p t (c i) -> p c t i", i=4),
+            ALU.subtract,
+        )
+        h_c = tile([P, O], U32, "h_c")
+        h_s = tile([P, O], U8, "h_s")
+        nc.vector.quantize_mx(out=h_c[:].bitcast(E5M2), scales=h_s[:], in_=h_bf[:].rearrange("p o t -> p (o t)"))
+
+        y = tile([P, PACK, O], F32, "y")
+        for t in range(PACK):
+            cols = slice(t * P, (t + 1) * P)
+            acc = ps.tile([P, O], F32, name="out%d" % t, tag="bank%d" % t)
+            nc.tensor.matmul_mx(
+                out=acc[:], lhsT=wb_c[:, cols].bitcast(E4M3), lhsT_scale=wb_s[:, cols],
+                rhs=h_c[:].bitcast(E5M2), rhs_scale=h_s[:], start=True, stop=True,
+            )
+            nc.vector.scalar_tensor_tensor(y[:, t, :], acc[:], gm_sb[:, t : t + 1], rs_sb[:, t, :], ALU.mult, ALU.add)
+        nc.sync.dma_start(out=dealt(out_0), in_=y[:])
+        y_bf = tile([P, O, PACK], BF16, "y_bf")
+        nc.vector.tensor_copy(
+            y_bf[:].rearrange("p (c i) t -> p c t i", i=4), y[:].rearrange("p t (c i) -> p c t i", i=4)
+        )
+        y_c = tile([P, O], U32, "y_c")
+        y_s = tile([P, O], U8, "y_s")
+        nc.vector.quantize_mx(out=y_c[:].bitcast(E4M3), scales=y_s[:], in_=y_bf[:].rearrange("p o t -> p (o t)"))
+        nc.sync.dma_start(out=out_1[0].rearrange("p c t -> p (c t)").bitcast(I32), in_=y_c[:].bitcast(I32))
+        for q in range(QUADS):
+            queue = nc.scalar if q % 2 == 0 else nc.sync
+            queue.dma_start(out=out_2[0, 4 * q : 4 * q + 4, :].bitcast(I32), in_=y_s[32 * q : 32 * q + 4, :].bitcast(I32))

@@ -69,6 +69,10 @@ def tile_list_looks_boundedgaps_gap_residual_pl_kernel(
         w_s = tile([P, R], U8, "w_s")
         wb_s = tile([P, N], U8, "wb_s")
 
+        warm_in = tile([P, 1], F32, "warm_in")
+        warm_out = tile([P, 1], F32, "warm_out")
+        nc.vector.memset(warm_in[:], 0.0)
+        nc.scalar.activation(warm_out[:], warm_in[:], ACT.Copy)
         nc.vector.memset(ws_raw[:].bitcast(I32), 0)
         nc.vector.memset(wbs_raw[:].bitcast(I32), 0)
 

@@ -37,8 +37,8 @@ def tile_list_looks_boundedgaps_gap_residual_pl_kernel(
         def dealt(ap):
             return ap.rearrange("(p t) c -> p t c", t=PACK)
 
-        def load_scales(queue, dst, src):
-            for q in range(QUADS):
+        def load_scales(queue, dst, src, quads):
+            for q in quads:
                 queue.dma_start(out=dst[32 * q : 32 * q + 4, :].bitcast(I32), in_=src[0, 4 * q : 4 * q + 4, :].bitcast(I32))
 
         def load_words(dst, src):
@@ -47,14 +47,23 @@ def tile_list_looks_boundedgaps_gap_residual_pl_kernel(
         def deal_words(dst, src):
             nc.scalar.copy(out=dst[:].rearrange("p (t m) -> p m t", t=PACK), in_=src[:].rearrange("p (m t) -> p m t", t=PACK))
 
-        def deal_scales(dst, src):
-            nc.vector.tensor_copy(out=dst[:].rearrange("p (t m) -> p t m", t=PACK), in_=src[:].rearrange("p (m t) -> p t m", t=PACK))
+        def deal_scales(engine, dst, src, first, count):
+            engine.tensor_copy(
+                out=dst[:].rearrange("p (t m) -> p t m", t=count),
+                in_=src[:].rearrange("p (m t) -> p t m", t=PACK)[:, first : first + count, :],
+            )
+
+        def woven(ap):
+            return ap.rearrange("p (c i) t -> p c t i", i=4)
+
+        def planar(ap):
+            return ap.rearrange("p t (c i) -> p c t i", i=4)
 
         la = tile([P, J // 16], U16, "la")
         lb = tile([P, J // 16], U16, "lb")
         l3 = tile([P, O // 16], U16, "l3")
         l4 = tile([P, O // 16], U16, "l4")
-        xa_sb = [tile([P, T], F32, "xa%d" % t) for t in range(PACK)]
+        xa_sb = [sb.tile([P, T], F32, name="xa%d" % t, tag="xa%d" % t, align_bytes=64) for t in range(PACK)]
         xb_sb = [tile([P, S], F32, "xb%d" % t) for t in range(PACK)]
         hb_sb = tile([P, PACK], F32, "hb_sb")
         fk_sb = tile([P, PACK], F32, "fk_sb")
@@ -62,96 +71,116 @@ def tile_list_looks_boundedgaps_gap_residual_pl_kernel(
         rs_sb = tile([P, PACK, O], F32, "rs_sb")
         w_raw = tile([P, R], U32, "w_raw")
         wb_raw = tile([P, N], U32, "wb_raw")
-        ws_raw = tile([P, R], U8, "ws_raw")
+        ws_raw = sb.tile([P, R], U8, name="ws_raw", tag="ws_raw", align_bytes=64)
         wbs_raw = tile([P, N], U8, "wbs_raw")
         w_c = tile([P, R], U32, "w_c")
-        wb_c = tile([P, N], U32, "wb_c")
-        w_s = tile([P, R], U8, "w_s")
-        wb_s = tile([P, N], U8, "wb_s")
 
         warm_in = tile([P, 1], F32, "warm_in")
         warm_out = tile([P, 1], F32, "warm_out")
         nc.vector.memset(warm_in[:], 0.0)
         nc.scalar.activation(warm_out[:], warm_in[:], ACT.Copy)
         nc.vector.memset(ws_raw[:].bitcast(I32), 0)
-        nc.vector.memset(wbs_raw[:].bitcast(I32), 0)
+        nc.gpsimd.memset(wbs_raw[:].bitcast(I32), 0)
 
         def load_vec(queue, dst, src):
             queue.dma_start(out=dst[:], in_=src.rearrange("(p t) c -> p (t c)", t=PACK))
 
-        load_vec(nc.gpsimd, gm_sb, gm)
-        for t in range(PACK):
-            if t == PACK - 1:
-                load_scales(nc.sync, ws_raw, w_scales)
-            nc.sync.dma_start(out=xb_sb[t][:], in_=dealt(xb)[:, t, :])
-            if t == 0:
-                nc.sync.dma_start(lb[:], offs2)
+        def load_xa(t):
             nc.sync.dma_start(out=xa_sb[t][:], in_=dealt(xa)[:, t, :])
-            if t == 0:
-                nc.sync.dma_start(la[:], offs)
-                load_vec(nc.sync, hb_sb, hb)
-                load_vec(nc.sync, fk_sb, fk)
+
+        def load_xb(t):
+            nc.sync.dma_start(out=xb_sb[t][:], in_=dealt(xb)[:, t, :])
+
+        load_scales(nc.gpsimd, wbs_raw, wb_scales, range(QUADS))
+        load_vec(nc.gpsimd, gm_sb, gm)
+        load_xb(0)
+        nc.sync.dma_start(lb[:], offs2)
+        load_vec(nc.sync, hb_sb, hb)
+        load_xa(0)
+        nc.sync.dma_start(la[:], offs)
+        load_vec(nc.sync, fk_sb, fk)
+        load_xb(1)
+        load_xa(1)
+        load_xb(2)
+        load_scales(nc.sync, ws_raw, w_scales, range(QUADS))
+        load_xa(2)
+        load_xb(3)
+        load_xa(3)
         load_words(w_raw, w_words)
         nc.sync.dma_start(l3[:], offs3)
         nc.sync.dma_start(l4[:], offs4)
-        load_scales(nc.sync, wbs_raw, wb_scales)
         load_words(wb_raw, wb_words)
         nc.sync.dma_start(out=rs_sb[:], in_=dealt(rs))
 
-        u_bf = [tile([P, HALF, PACK], BF16, "u_bf%d" % h) for h in range(2)]
+        halves = [slice(0, HALF), slice(HALF, J)]
+        u_bf = sb.tile([P, J, PACK], BF16, name="u_bf", tag="u_bf", align_bytes=64)
         for t in range(PACK):
             gb = tile([P, J], F32, "gb%d" % t)
+            ga = tile([P, J], F32, "ga%d" % t)
+            neg = tile([P, J], F32, "neg%d" % t)
             nc.scalar.activation(gb[:], xb_sb[t][:].indirect(lb[:]), ACT.Copy)
-            ga = [tile([P, HALF], F32, "ga%d_%d" % (t, h)) for h in range(2)]
-            nc.scalar.activation(ga[0][:], xa_sb[t][:].indirect(la[:, 0:COLS]), ACT.Copy)
-            if t % 2 == 1:
-                nc.vector.tensor_copy(ga[1][:], xa_sb[t][:].indirect(la[:, COLS : 2 * COLS]))
+            if t == 0:
+                nc.scalar.activation(ga[:, halves[0]], xa_sb[t][:].indirect(la[:, 0:COLS]), ACT.Copy)
+                nc.vector.tensor_copy(ga[:, halves[1]], xa_sb[t][:].indirect(la[:, COLS : 2 * COLS]))
             else:
-                nc.scalar.activation(ga[1][:], xa_sb[t][:].indirect(la[:, COLS : 2 * COLS]), ACT.Copy)
-            neg = [tile([P, HALF], F32, "neg%d_%d" % (t, h)) for h in range(2)]
-            for h in range(2):
-                nc.vector.scalar_tensor_tensor(
-                    neg[h][:], gb[:, h * HALF : (h + 1) * HALF], hb_sb[:, t : t + 1], ga[h][:], ALU.min, ALU.subtract
-                )
-            for h in range(2):
-                nc.vector.tensor_scalar(u_bf[h][:, :, t], neg[h][:], fk_sb[:, t : t + 1], -1.0, ALU.mult, ALU.mult)
+                nc.scalar.activation(ga[:], xa_sb[t][:].indirect(la[:]), ACT.Copy)
+            pieces = halves if t == PACK - 1 else [slice(0, J)]
+            for js in pieces:
+                nc.vector.scalar_tensor_tensor(neg[:, js], gb[:, js], hb_sb[:, t : t + 1], ga[:, js], ALU.min, ALU.subtract)
             if t == PACK - 2:
-                deal_scales(w_s, ws_raw)
+                w_s_lo = sb.tile([P, R // 2], U8, name="w_s_lo", tag="xa%d" % t, align_bytes=64)
+                deal_scales(nc.vector, w_s_lo, ws_raw, 0, 2)
+            for js in pieces:
+                nc.vector.tensor_scalar(u_bf[:, js, t], neg[:, js], fk_sb[:, t : t + 1], -1.0, ALU.mult, ALU.mult)
         deal_words(w_c, w_raw)
         u_c = [tile([P, HALF], U32, "u_c%d" % h) for h in range(2)]
         u_s = [tile([P, HALF], U8, "u_s%d" % h) for h in range(2)]
         for h in range(2):
-            nc.vector.quantize_mx(out=u_c[h][:].bitcast(E5M2), scales=u_s[h][:], in_=u_bf[h][:].rearrange("p j t -> p (j t)"))
-        deal_scales(wb_s, wbs_raw)
-        deal_words(wb_c, wb_raw)
+            nc.vector.quantize_mx(out=u_c[h][:].bitcast(E5M2), scales=u_s[h][:], in_=u_bf[:, halves[h], :].rearrange("p j t -> p (j t)"))
+        w_s_hi = sb.tile([P, R // 2], U8, name="w_s_hi", tag="u_bf", align_bytes=64)
+        deal_scales(nc.vector, w_s_hi, ws_raw, 2, 2)
+        w_s = [w_s_lo[:, 0:P], w_s_lo[:, P : 2 * P], w_s_hi[:, 0:P], w_s_hi[:, P : 2 * P]]
+        wb_s = sb.tile([P, N], U8, name="wb_s", tag="ws_raw", align_bytes=64)
+        deal_scales(nc.gpsimd, wb_s, wbs_raw, 0, PACK)
 
         g3 = tile([P, PACK, O], F32, "g3")
         g4 = tile([P, PACK, O], F32, "g4")
-        for t in range(PACK):
+        ha = [sb.tile([P, J], F32, name="ha%d" % t, tag="ha%d" % t, align_bytes=64) for t in range(PACK)]
+
+        def product(t):
             cols = slice(t * P, (t + 1) * P)
-            ha = tile([P, J], F32, "ha%d" % t)
             for h in range(2):
                 acc = ps.tile([P, HALF], F32, name="acc%d_%d" % (t, h), tag="bank%d" % (2 * t + h))
                 nc.tensor.matmul_mx(
-                    out=acc[:], lhsT=w_c[:, cols].bitcast(E5M2), lhsT_scale=w_s[:, cols],
+                    out=acc[:], lhsT=w_c[:, cols].bitcast(E5M2), lhsT_scale=w_s[t],
                     rhs=u_c[h][:].bitcast(E5M2), rhs_scale=u_s[h][:], start=True, stop=True,
                 )
                 if h == 0:
-                    nc.vector.tensor_scalar_max(ha[:, 0:HALF], acc[:], 0.0)
+                    nc.vector.tensor_scalar_max(ha[t][:, 0:HALF], acc[:], 0.0)
                 else:
-                    nc.scalar.activation(ha[:, HALF:J], acc[:], ACT.Relu)
-            nc.vector.tensor_copy(g3[:, t, :], ha[:].indirect(l3[:]))
-            nc.scalar.activation(g4[:, t, :], ha[:].indirect(l4[:]), ACT.Copy)
-        h_bf = tile([P, O, PACK], BF16, "h_bf")
-        nc.vector.tensor_tensor(
-            h_bf[:].rearrange("p (c i) t -> p c t i", i=4),
-            g3[:].rearrange("p t (c i) -> p c t i", i=4),
-            g4[:].rearrange("p t (c i) -> p c t i", i=4),
-            ALU.subtract,
-        )
+                    nc.scalar.activation(ha[t][:, HALF:J], acc[:], ACT.Relu)
+
+        def look_up(t):
+            nc.vector.tensor_copy(g3[:, t, :], ha[t][:].indirect(l3[:]))
+            nc.scalar.activation(g4[:, t, :], ha[t][:].indirect(l4[:]), ACT.Copy)
+
+        for step in range(PACK + 1):
+            if step < PACK:
+                product(step)
+            if step > 0:
+                look_up(step - 1)
+        wb_c = sb.tile([P, N], U32, name="wb_c", tag="ha%d" % (PACK - 1), align_bytes=64)
+        deal_words(wb_c, wb_raw)
+        places = [slice(0, O // 2), slice(O // 2, O)]
+        h_bf = [tile([P, O // 2, PACK], BF16, "h_bf%d" % h) for h in range(2)]
         h_c = tile([P, O], U32, "h_c")
         h_s = tile([P, O], U8, "h_s")
-        nc.vector.quantize_mx(out=h_c[:].bitcast(E5M2), scales=h_s[:], in_=h_bf[:].rearrange("p o t -> p (o t)"))
+        for h in range(2):
+            nc.vector.tensor_tensor(woven(h_bf[h][:]), planar(g3[:, :, places[h]]), planar(g4[:, :, places[h]]), ALU.subtract)
+        for h in range(2):
+            nc.vector.quantize_mx(
+                out=h_c[:, places[h]].bitcast(E5M2), scales=h_s[:, places[h]], in_=h_bf[h][:].rearrange("p o t -> p (o t)")
+            )
 
         y = tile([P, PACK, O], F32, "y")
         for t in range(PACK):
@@ -161,15 +190,18 @@ def tile_list_looks_boundedgaps_gap_residual_pl_kernel(
                 out=acc[:], lhsT=wb_c[:, cols].bitcast(E4M3), lhsT_scale=wb_s[:, cols],
                 rhs=h_c[:].bitcast(E5M2), rhs_scale=h_s[:], start=True, stop=True,
             )
-            nc.vector.scalar_tensor_tensor(y[:, t, :], acc[:], gm_sb[:, t : t + 1], rs_sb[:, t, :], ALU.mult, ALU.add)
+            for oc in places if t == PACK - 1 else [slice(0, O)]:
+                nc.vector.scalar_tensor_tensor(y[:, t, oc], acc[:, oc], gm_sb[:, t : t + 1], rs_sb[:, t, oc], ALU.mult, ALU.add)
         nc.sync.dma_start(out=dealt(out_0), in_=y[:])
-        y_bf = tile([P, O, PACK], BF16, "y_bf")
-        nc.vector.tensor_copy(
-            y_bf[:].rearrange("p (c i) t -> p c t i", i=4), y[:].rearrange("p t (c i) -> p c t i", i=4)
-        )
+        y_bf = [tile([P, O // 2, PACK], BF16, "y_bf%d" % h) for h in range(2)]
         y_c = tile([P, O], U32, "y_c")
         y_s = tile([P, O], U8, "y_s")
-        nc.vector.quantize_mx(out=y_c[:].bitcast(E4M3), scales=y_s[:], in_=y_bf[:].rearrange("p o t -> p (o t)"))
+        for h in range(2):
+            nc.vector.tensor_copy(woven(y_bf[h][:]), planar(y[:, :, places[h]]))
+        for h in range(2):
+            nc.vector.quantize_mx(
+                out=y_c[:, places[h]].bitcast(E4M3), scales=y_s[:, places[h]], in_=y_bf[h][:].rearrange("p o t -> p (o t)")
+            )
         nc.sync.dma_start(out=out_1[0].rearrange("p c t -> p (c t)").bitcast(I32), in_=y_c[:].bitcast(I32))
         for q in range(QUADS):
             queue = nc.scalar if q % 2 == 0 else nc.sync

@@ -79,8 +79,8 @@ def tile_list_looks_boundedgaps_gap_residual_pl_kernel(
         warm_out = tile([P, 1], F32, "warm_out")
         nc.vector.memset(warm_in[:], 0.0)
         nc.scalar.activation(warm_out[:], warm_in[:], ACT.Copy)
-        nc.vector.memset(ws_raw[:].bitcast(I32), 0)
-        nc.gpsimd.memset(wbs_raw[:].bitcast(I32), 0)
+        nc.gpsimd.memset(ws_raw[:].bitcast(I32), 0)
+        nc.vector.memset(wbs_raw[:].bitcast(I32), 0)
 
         def load_vec(queue, dst, src):
             queue.dma_start(out=dst[:], in_=src.rearrange("(p t) c -> p (t c)", t=PACK))
@@ -91,7 +91,7 @@ def tile_list_looks_boundedgaps_gap_residual_pl_kernel(
         def load_xb(t):
             nc.sync.dma_start(out=xb_sb[t][:], in_=dealt(xb)[:, t, :])
 
-        load_scales(nc.gpsimd, wbs_raw, wb_scales, range(QUADS))
+        load_scales(nc.gpsimd, ws_raw, w_scales, (0, 1))
         load_vec(nc.gpsimd, gm_sb, gm)
         load_xb(0)
         nc.sync.dma_start(lb[:], offs2)
@@ -102,13 +102,14 @@ def tile_list_looks_boundedgaps_gap_residual_pl_kernel(
         load_xb(1)
         load_xa(1)
         load_xb(2)
-        load_scales(nc.sync, ws_raw, w_scales, range(QUADS))
+        load_scales(nc.sync, ws_raw, w_scales, (2, 3))
         load_xa(2)
         load_xb(3)
         load_xa(3)
         load_words(w_raw, w_words)
         nc.sync.dma_start(l3[:], offs3)
         nc.sync.dma_start(l4[:], offs4)
+        load_scales(nc.sync, wbs_raw, wb_scales, range(QUADS))
         load_words(wb_raw, wb_words)
         nc.sync.dma_start(out=rs_sb[:], in_=dealt(rs))
 
@@ -122,6 +123,9 @@ def tile_list_looks_boundedgaps_gap_residual_pl_kernel(
             if t == 0:
                 nc.scalar.activation(ga[:, halves[0]], xa_sb[t][:].indirect(la[:, 0:COLS]), ACT.Copy)
                 nc.vector.tensor_copy(ga[:, halves[1]], xa_sb[t][:].indirect(la[:, COLS : 2 * COLS]))
+            elif t == PACK - 1:
+                for h in range(2):
+                    nc.scalar.activation(ga[:, halves[h]], xa_sb[t][:].indirect(la[:, h * COLS : (h + 1) * COLS]), ACT.Copy)
             else:
                 nc.scalar.activation(ga[:], xa_sb[t][:].indirect(la[:]), ACT.Copy)
             pieces = halves if t == PACK - 1 else [slice(0, J)]
@@ -161,8 +165,12 @@ def tile_list_looks_boundedgaps_gap_residual_pl_kernel(
                     nc.scalar.activation(ha[t][:, HALF:J], acc[:], ACT.Relu)
 
         def look_up(t):
-            nc.vector.tensor_copy(g3[:, t, :], ha[t][:].indirect(l3[:]))
-            nc.scalar.activation(g4[:, t, :], ha[t][:].indirect(l4[:]), ACT.Copy)
+            parts = 2 if t == PACK - 1 else 1
+            for h in range(parts):
+                oc = slice(h * O // parts, (h + 1) * O // parts)
+                lc = slice(oc.start // 16, oc.stop // 16)
+                nc.vector.tensor_copy(g3[:, t, oc], ha[t][:].indirect(l3[:, lc]))
+                nc.scalar.activation(g4[:, t, oc], ha[t][:].indirect(l4[:, lc]), ACT.Copy)
 
         for step in range(PACK + 1):
             if step < PACK:

from contextlib import ExitStack

import concourse.mybir as mybir

K, T, J, S, R, O, N = 512, 512, 256, 512, 512, 128, 512
FLOPS = 2 * K * R * J + 2 * R * N * O

F32 = mybir.dt.float32
BF16 = mybir.dt.bfloat16
I32 = mybir.dt.int32
U32 = mybir.dt.uint32
U16 = mybir.dt.uint16
U8 = mybir.dt.uint8
E4M3 = mybir.dt.float8_e4m3fn_x4
E5M2 = mybir.dt.float8_e5m2_x4
ALU = mybir.AluOpType
ACT = mybir.ActivationFunctionType

P = 128
PACK = 4
QUADS = 4
HALF = J // 2
COLS = HALF // 16


def tile_list_looks_boundedgaps_gap_residual_pl_kernel(
    tc, xa, xb, hb, fk, w_words, w_scales, wb_words, wb_scales, rs, gm, offs, offs2, offs3, offs4, out_0, out_1, out_2
):
    nc = tc.nc
    with ExitStack() as ctx:
        sb = ctx.enter_context(tc.tile_pool(name="sb", bufs=1))
        ps = ctx.enter_context(tc.psum_pool(name="ps", bufs=1))

        def tile(shape, dtype, name):
            return sb.tile(shape, dtype, name=name, align_bytes=64)

        def dealt(ap):
            return ap.rearrange("(p t) c -> p t c", t=PACK)

        def load_scales(queue, dst, src, quads):
            for q in quads:
                queue.dma_start(out=dst[32 * q : 32 * q + 4, :].bitcast(I32), in_=src[0, 4 * q : 4 * q + 4, :].bitcast(I32))

        def load_words(dst, src):
            nc.sync.dma_start(out=dst[:].bitcast(I32), in_=src[0].rearrange("p c t -> p (c t)").bitcast(I32))

        def deal_words(dst, src):
            nc.scalar.copy(out=dst[:].rearrange("p (t m) -> p m t", t=PACK), in_=src[:].rearrange("p (m t) -> p m t", t=PACK))

        def deal_scales(engine, dst, src, first, count):
            engine.tensor_copy(
                out=dst[:].rearrange("p (t m) -> p t m", t=count),
                in_=src[:].rearrange("p (m t) -> p t m", t=PACK)[:, first : first + count, :],
            )

        def woven(ap):
            return ap.rearrange("p (c i) t -> p c t i", i=4)

        def planar(ap):
            return ap.rearrange("p t (c i) -> p c t i", i=4)

        la = tile([P, J // 16], U16, "la")
        lb = tile([P, J // 16], U16, "lb")
        l3 = tile([P, O // 16], U16, "l3")
        l4 = tile([P, O // 16], U16, "l4")
        xa_sb = [sb.tile([P, T], F32, name="xa%d" % t, tag="xa%d" % t, align_bytes=64) for t in range(PACK)]
        xb_sb = [tile([P, S], F32, "xb%d" % t) for t in range(PACK)]
        hb_sb = tile([P, PACK], F32, "hb_sb")
        fk_sb = tile([P, PACK], F32, "fk_sb")
        gm_sb = tile([P, PACK], F32, "gm_sb")
        rs_sb = tile([P, PACK, O], F32, "rs_sb")
        w_raw = tile([P, R], U32, "w_raw")
        wb_raw = tile([P, N], U32, "wb_raw")
        ws_raw = sb.tile([P, R], U8, name="ws_raw", tag="ws_raw", align_bytes=64)
        wbs_raw = tile([P, N], U8, "wbs_raw")
        w_c = tile([P, R], U32, "w_c")

        warm_in = tile([P, 1], F32, "warm_in")
        warm_out = tile([P, 1], F32, "warm_out")
        nc.vector.memset(warm_in[:], 0.0)
        nc.scalar.activation(warm_out[:], warm_in[:], ACT.Copy)
        nc.gpsimd.memset(ws_raw[:].bitcast(I32), 0)
        nc.vector.memset(wbs_raw[:].bitcast(I32), 0)

        def load_vec(queue, dst, src):
            queue.dma_start(out=dst[:], in_=src.rearrange("(p t) c -> p (t c)", t=PACK))

        def load_xa(t):
            nc.sync.dma_start(out=xa_sb[t][:], in_=dealt(xa)[:, t, :])

        def load_xb(t):
            nc.sync.dma_start(out=xb_sb[t][:], in_=dealt(xb)[:, t, :])

        load_scales(nc.gpsimd, ws_raw, w_scales, (0, 1))
        load_vec(nc.gpsimd, gm_sb, gm)
        load_xb(0)
        nc.sync.dma_start(lb[:], offs2)
        load_vec(nc.sync, hb_sb, hb)
        load_xa(0)
        nc.sync.dma_start(la[:], offs)
        load_vec(nc.sync, fk_sb, fk)
        load_xb(1)
        load_xa(1)
        load_xb(2)
        load_scales(nc.sync, ws_raw, w_scales, (2, 3))
        load_xa(2)
        load_xb(3)
        load_xa(3)
        load_words(w_raw, w_words)
        nc.sync.dma_start(l3[:], offs3)
        nc.sync.dma_start(l4[:], offs4)
        load_scales(nc.sync, wbs_raw, wb_scales, range(QUADS))
        load_words(wb_raw, wb_words)
        nc.sync.dma_start(out=rs_sb[:], in_=dealt(rs))

        halves = [slice(0, HALF), slice(HALF, J)]
        u_bf = sb.tile([P, J, PACK], BF16, name="u_bf", tag="u_bf", align_bytes=64)
        for t in range(PACK):
            gb = tile([P, J], F32, "gb%d" % t)
            ga = tile([P, J], F32, "ga%d" % t)
            neg = tile([P, J], F32, "neg%d" % t)
            nc.scalar.activation(gb[:], xb_sb[t][:].indirect(lb[:]), ACT.Copy)
            if t == 0:
                nc.scalar.activation(ga[:, halves[0]], xa_sb[t][:].indirect(la[:, 0:COLS]), ACT.Copy)
                nc.vector.tensor_copy(ga[:, halves[1]], xa_sb[t][:].indirect(la[:, COLS : 2 * COLS]))
            elif t == PACK - 1:
                for h in range(2):
                    nc.scalar.activation(ga[:, halves[h]], xa_sb[t][:].indirect(la[:, h * COLS : (h + 1) * COLS]), ACT.Copy)
            else:
                nc.scalar.activation(ga[:], xa_sb[t][:].indirect(la[:]), ACT.Copy)
            pieces = halves if t == PACK - 1 else [slice(0, J)]
            for js in pieces:
                nc.vector.scalar_tensor_tensor(neg[:, js], gb[:, js], hb_sb[:, t : t + 1], ga[:, js], ALU.min, ALU.subtract)
            if t == PACK - 2:
                w_s_lo = sb.tile([P, R // 2], U8, name="w_s_lo", tag="xa%d" % t, align_bytes=64)
                deal_scales(nc.vector, w_s_lo, ws_raw, 0, 2)
            for js in pieces:
                nc.vector.tensor_scalar(u_bf[:, js, t], neg[:, js], fk_sb[:, t : t + 1], -1.0, ALU.mult, ALU.mult)
        deal_words(w_c, w_raw)
        u_c = [tile([P, HALF], U32, "u_c%d" % h) for h in range(2)]
        u_s = [tile([P, HALF], U8, "u_s%d" % h) for h in range(2)]
        for h in range(2):
            nc.vector.quantize_mx(out=u_c[h][:].bitcast(E5M2), scales=u_s[h][:], in_=u_bf[:, halves[h], :].rearrange("p j t -> p (j t)"))
        w_s_hi = sb.tile([P, R // 2], U8, name="w_s_hi", tag="u_bf", align_bytes=64)
        deal_scales(nc.vector, w_s_hi, ws_raw, 2, 2)
        w_s = [w_s_lo[:, 0:P], w_s_lo[:, P : 2 * P], w_s_hi[:, 0:P], w_s_hi[:, P : 2 * P]]
        wb_s = sb.tile([P, N], U8, name="wb_s", tag="ws_raw", align_bytes=64)
        deal_scales(nc.gpsimd, wb_s, wbs_raw, 0, PACK)

        g3 = tile([P, PACK, O], F32, "g3")
        g4 = tile([P, PACK, O], F32, "g4")
        ha = [sb.tile([P, J], F32, name="ha%d" % t, tag="ha%d" % t, align_bytes=64) for t in range(PACK)]

        def product(t):
            cols = slice(t * P, (t + 1) * P)
            for h in range(2):
                acc = ps.tile([P, HALF], F32, name="acc%d_%d" % (t, h), tag="bank%d" % (2 * t + h))
                nc.tensor.matmul_mx(
                    out=acc[:], lhsT=w_c[:, cols].bitcast(E5M2), lhsT_scale=w_s[t],
                    rhs=u_c[h][:].bitcast(E5M2), rhs_scale=u_s[h][:], start=True, stop=True,
                )
                if h == 0:
                    nc.vector.tensor_scalar_max(ha[t][:, 0:HALF], acc[:], 0.0)
                else:
                    nc.scalar.activation(ha[t][:, HALF:J], acc[:], ACT.Relu)

        def look_up(t):
            parts = 2 if t == PACK - 1 else 1
            for h in range(parts):
                oc = slice(h * O // parts, (h + 1) * O // parts)
                lc = slice(oc.start // 16, oc.stop // 16)
                nc.vector.tensor_copy(g3[:, t, oc], ha[t][:].indirect(l3[:, lc]))
                nc.scalar.activation(g4[:, t, oc], ha[t][:].indirect(l4[:, lc]), ACT.Copy)

        for step in range(PACK + 1):
            if step < PACK:
                product(step)
            if step > 0:
                look_up(step - 1)
        wb_c = sb.tile([P, N], U32, name="wb_c", tag="ha%d" % (PACK - 1), align_bytes=64)
        deal_words(wb_c, wb_raw)
        places = [slice(0, O // 2), slice(O // 2, O)]
        h_bf = [tile([P, O // 2, PACK], BF16, "h_bf%d" % h) for h in range(2)]
        h_c = tile([P, O], U32, "h_c")
        h_s = tile([P, O], U8, "h_s")
        for h in range(2):
            nc.vector.tensor_tensor(woven(h_bf[h][:]), planar(g3[:, :, places[h]]), planar(g4[:, :, places[h]]), ALU.subtract)
        for h in range(2):
            nc.vector.quantize_mx(
                out=h_c[:, places[h]].bitcast(E5M2), scales=h_s[:, places[h]], in_=h_bf[h][:].rearrange("p o t -> p (o t)")
            )

        y = tile([P, PACK, O], F32, "y")
        for t in range(PACK):
            cols = slice(t * P, (t + 1) * P)
            acc = ps.tile([P, O], F32, name="out%d" % t, tag="bank%d" % t)
            nc.tensor.matmul_mx(
                out=acc[:], lhsT=wb_c[:, cols].bitcast(E4M3), lhsT_scale=wb_s[:, cols],
                rhs=h_c[:].bitcast(E5M2), rhs_scale=h_s[:], start=True, stop=True,
            )
            for oc in places if t == PACK - 1 else [slice(0, O)]:
                nc.vector.scalar_tensor_tensor(y[:, t, oc], acc[:, oc], gm_sb[:, t : t + 1], rs_sb[:, t, oc], ALU.mult, ALU.add)
        nc.sync.dma_start(out=dealt(out_0), in_=y[:])
        y_bf = [tile([P, O // 2, PACK], BF16, "y_bf%d" % h) for h in range(2)]
        y_c = tile([P, O], U32, "y_c")
        y_s = tile([P, O], U8, "y_s")
        for h in range(2):
            nc.vector.tensor_copy(woven(y_bf[h][:]), planar(y[:, :, places[h]]))
        for h in range(2):
            nc.vector.quantize_mx(
                out=y_c[:, places[h]].bitcast(E4M3), scales=y_s[:, places[h]], in_=y_bf[h][:].rearrange("p o t -> p (o t)")
            )
        nc.sync.dma_start(out=out_1[0].rearrange("p c t -> p (c t)").bitcast(I32), in_=y_c[:].bitcast(I32))
        for q in range(QUADS):
            queue = nc.scalar if q % 2 == 0 else nc.sync
            queue.dma_start(out=out_2[0, 4 * q : 4 * q + 4, :].bitcast(I32), in_=y_s[32 * q : 32 * q + 4, :].bitcast(I32))
